import numpy as np
import ml_dtypes


def mxq(x, axis, fmt="e4m3"):
    dtype, down = {"e4m3": (ml_dtypes.float8_e4m3fn, 7), "e5m2": (ml_dtypes.float8_e5m2, 14)}[fmt]
    v = np.moveaxis(np.asarray(x, np.float32).astype(ml_dtypes.bfloat16).astype(np.float64), axis, -1)
    blocks = v.reshape(v.shape[:-1] + (-1, 32))
    amax = np.abs(blocks).max(-1, keepdims=True)
    byte = np.maximum(np.where(amax > 0, np.frexp(amax)[1] - 1 + 127, 0) - down, 1)
    scale = np.exp2(byte - 127.0)
    codes = (blocks / scale).astype(np.float32).astype(dtype).astype(np.float64)
    return np.moveaxis((codes * scale).reshape(v.shape), -1, axis)


WIDE = False


def mx_kscale(k, group=512):
    if not WIDE:
        return np.ones(k)
    levels = np.array([18, -18])
    if group != 512:
        return np.exp2(np.random.permutation(np.resize(levels, k // group))).repeat(group)
    if k % 512:
        return np.exp2(np.random.permutation(np.resize(levels, k // 32))).repeat(32)
    a = np.empty((k // 512, 16))
    for p in range(k // 512):
        a[p, :8] = np.random.permutation(np.resize(levels, 8))
        for g in range(8):
            far = levels[np.abs(levels - a[p, g]) >= 10]
            a[p, g + 8] = far[np.random.randint(len(far))]
    return np.exp2(a.ravel()).repeat(32)


def f64(x):
    return np.asarray(x).astype(np.float64)


G, D, M, N = 8, 128, 128, 512


def setup_inputs():
    n = np.random.standard_normal
    s = mx_kscale(D, 0)[:, None]
    return {
        "x": (n((G, D, N)) * s).astype(np.float32),
        "w": (n((G, D, M)) / np.sqrt(D) / s).astype(np.float32),
        "b": (0.5 * n((G, M, 1))).astype(np.float32),
        "r": n((G, M, N)).astype(np.float32),
    }


def reference(x, w, b, r):
    xq = mxq(f64(x), 1, "e4m3")
    y = mxq(f64(w), 1, "e4m3").transpose(0, 2, 1) @ xq
    y = y + f64(b)
    y = np.maximum(y, 0.0)
    y = y + f64(r)
    return y

@@ -1,0 +1,125 @@
+from contextlib import ExitStack
+
+import concourse.mybir as mybir
+
+G, D, M, N = 8, 128, 128, 512
+FLOPS = 2 * G * D * M * N
+
+F32 = mybir.dt.float32
+BF16 = mybir.dt.bfloat16
+U32 = mybir.dt.uint32
+U8 = mybir.dt.uint8
+FP8X4 = mybir.dt.float8_e4m3fn_x4
+RELU = mybir.ActivationFunctionType.Relu
+ADD = mybir.AluOpType.add
+
+P = 128
+PACK = 4
+ROWS = D // PACK
+SIDE = P // ROWS
+SETS = G // SIDE
+QUAD = 32
+RUN = 4
+X_VECTOR_COLS = 344
+PAIR = 2
+
+
+def interleave(copy, grouped, raw, cols):
+    copy(
+        out=grouped[:, cols, :].rearrange("p (c i) j -> p c j i", i=RUN),
+        in_=raw[:, :, cols].rearrange("p j (c i) -> p c j i", i=RUN),
+    )
+
+
+def tile_rows_glin_relu_bias_res_kernel(tc, x, w, b, r, out):
+    nc = tc.nc
+    x_rows = x.flatten_outer_dims().rearrange("(s q j) n -> s q j n", s=SETS, j=PACK)
+    w_rows = w.flatten_outer_dims().rearrange("(s q j) m -> q s j m", s=SETS, j=PACK)
+    b_rows = b.rearrange("g m one -> g (m one)")
+    r_rows = r.rearrange("g m n -> m g n")
+    out_rows = out.rearrange("g m n -> m g n")
+
+    with ExitStack() as ctx:
+        sb = ctx.enter_context(tc.tile_pool(name="sb", bufs=1))
+        psum = ctx.enter_context(tc.psum_pool(name="psum", bufs=1))
+        ctx.enter_context(tc.manual_schedule())
+
+        x_raw = [sb.tile([P, PACK, N], F32, name="x_raw%d" % s, align_bytes=64) for s in range(SETS)]
+        x_bf = [sb.tile([P, N, PACK], BF16, name="x_bf%d" % s, align_bytes=64) for s in range(SETS)]
+        x_codes = [sb.tile([P, N], U32, name="x_codes%d" % s, align_bytes=64) for s in range(SETS)]
+        x_scales = [sb.tile([P, N], U8, name="x_scales%d" % s, align_bytes=64) for s in range(SETS)]
+        w_raw = sb.tile([P, SETS, PACK, M], F32, align_bytes=64)
+        w_bf = [sb.tile([P, M, PACK], BF16, name="w_bf%d" % s, align_bytes=64) for s in range(SETS)]
+        w_codes = [sb.tile([P, M], U32, name="w_codes%d" % s, align_bytes=64) for s in range(SETS)]
+        w_scales = [sb.tile([P, M], U8, name="w_scales%d" % s, align_bytes=64) for s in range(SETS)]
+        b_blocks = sb.tile([P, QUAD], F32, align_bytes=64)
+        bias = sb.tile([P, QUAD], F32, align_bytes=64)
+        r_sb = [sb.tile([P, PAIR, N], F32, name="r_sb%d" % k, align_bytes=64) for k in range(G // PAIR)]
+        act = [sb.tile([P, N], F32, name="act%d" % g, align_bytes=64) for g in range(G)]
+        res = [sb.tile([P, PAIR, N], F32, name="res%d" % k, align_bytes=64) for k in range(G // PAIR)]
+        acc = [psum.tile([M, N], F32, name="acc%d" % g) for g in range(G)]
+
+        def quantize(codes, scales, grouped):
+            nc.vector.quantize_mx(
+                out=codes[:].bitcast(FP8X4),
+                scales=scales[:],
+                in_=grouped[:].rearrange("p c j -> p (c j)"),
+            )
+
+        def products(s):
+            for c in range(SIDE):
+                rows = slice(ROWS * c, ROWS * (c + 1))
+                nc.tensor.matmul_mx(
+                    out=acc[SIDE * s + c][:],
+                    lhsT=w_codes[s][rows, :].bitcast(FP8X4),
+                    lhsT_scale=w_scales[s][rows, :],
+                    rhs=x_codes[s][rows, :].bitcast(FP8X4),
+                    rhs_scale=x_scales[s][rows, :],
+                    start=True,
+                    stop=True,
+                )
+
+        def bias_relu(g):
+            nc.scalar.activation(out=act[g][:], in_=acc[g][:], func=RELU, bias=bias[:, g : g + 1])
+
+        vector_cols = slice(0, X_VECTOR_COLS)
+        scalar_cols = slice(X_VECTOR_COLS, N)
+        all_m = slice(0, M)
+
+        nc.sync.dma_start(out=x_raw[0][:], in_=x_rows[0])
+        nc.sync.dma_start(out=w_raw[:], in_=w_rows)
+        nc.sync.dma_start(out=x_raw[1][:], in_=x_rows[1])
+
+        nc.vector.memset(b_blocks[:], 0.0)
+        for q in range(P // QUAD):
+            nc.scalar.dma_start(
+                out=b_blocks[QUAD * q : QUAD * q + G, :],
+                in_=b_rows[:, QUAD * q : QUAD * (q + 1)],
+            )
+
+        for k in range(G // PAIR):
+            nc.sync.dma_start(out=r_sb[k][:], in_=r_rows[:, PAIR * k : PAIR * (k + 1), :])
+
+        interleave(nc.vector.tensor_copy, x_bf[0], x_raw[0], vector_cols)
+        interleave(nc.scalar.copy, x_bf[0], x_raw[0], scalar_cols)
+        quantize(x_codes[0], x_scales[0], x_bf[0])
+        for s in range(SETS):
+            interleave(nc.scalar.copy, w_bf[s], w_raw[:, s, :, :], all_m)
+        quantize(w_codes[0], w_scales[0], w_bf[0])
+        nc.vector.transpose(out=bias[:], in_=b_blocks[:])
+        quantize(w_codes[1], w_scales[1], w_bf[1])
+        products(0)
+        bias_relu(0)
+
+        interleave(nc.vector.tensor_copy, x_bf[1], x_raw[1], vector_cols)
+        interleave(nc.scalar.copy, x_bf[1], x_raw[1], scalar_cols)
+        quantize(x_codes[1], x_scales[1], x_bf[1])
+        products(1)
+        for g in range(1, G):
+            bias_relu(g)
+
+        for g in range(G):
+            k, e = divmod(g, PAIR)
+            nc.vector.tensor_tensor(out=res[k][:, e, :], in0=act[g][:], in1=r_sb[k][:, e, :], op=ADD)
+            if e == PAIR - 1:
+                nc.sync.dma_start(out=out_rows[:, PAIR * k : PAIR * (k + 1), :], in_=res[k][:])

@@ -35,7 +35,7 @@ def tile_rows_glin_relu_bias_res_kernel(tc, x, w, b, r, out):
     nc = tc.nc
     x_rows = x.flatten_outer_dims().rearrange("(s q j) n -> s q j n", s=SETS, j=PACK)
     w_rows = w.flatten_outer_dims().rearrange("(s q j) m -> q s j m", s=SETS, j=PACK)
-    b_rows = b.rearrange("g m one -> g (m one)")
+    b_rows = b.rearrange("g (q i) one -> q g (i one)", i=QUAD)
     r_rows = r.rearrange("g m n -> m g n")
     out_rows = out.rearrange("g m n -> m g n")
 
@@ -52,8 +52,8 @@ def tile_rows_glin_relu_bias_res_kernel(tc, x, w, b, r, out):
         w_bf = [sb.tile([P, M, PACK], BF16, name="w_bf%d" % s, align_bytes=64) for s in range(SETS)]
         w_codes = [sb.tile([P, M], U32, name="w_codes%d" % s, align_bytes=64) for s in range(SETS)]
         w_scales = [sb.tile([P, M], U8, name="w_scales%d" % s, align_bytes=64) for s in range(SETS)]
-        b_blocks = sb.tile([P, QUAD], F32, align_bytes=64)
-        bias = sb.tile([P, QUAD], F32, align_bytes=64)
+        b_blocks = sb.tile([P, G, QUAD], F32, align_bytes=64)
+        bias = sb.tile([P, G, QUAD], F32, align_bytes=64)
         r_sb = [sb.tile([P, PAIR, N], F32, name="r_sb%d" % k, align_bytes=64) for k in range(G // PAIR)]
         act = [sb.tile([P, N], F32, name="act%d" % g, align_bytes=64) for g in range(G)]
         res = [sb.tile([P, PAIR, N], F32, name="res%d" % k, align_bytes=64) for k in range(G // PAIR)]
@@ -80,23 +80,17 @@ def tile_rows_glin_relu_bias_res_kernel(tc, x, w, b, r, out):
                 )
 
         def bias_relu(g):
-            nc.scalar.activation(out=act[g][:], in_=acc[g][:], func=RELU, bias=bias[:, g : g + 1])
+            nc.scalar.activation(out=act[g][:], in_=acc[g][:], func=RELU, bias=bias[:, g, 0:1])
 
         vector_cols = slice(0, X_VECTOR_COLS)
         scalar_cols = slice(X_VECTOR_COLS, N)
         all_m = slice(0, M)
 
+        nc.vector.memset(b_blocks[:], 0.0)
         nc.sync.dma_start(out=x_raw[0][:], in_=x_rows[0])
+        nc.sync.dma_start(out=b_blocks[0:P:QUAD, :, :], in_=b_rows)
         nc.sync.dma_start(out=w_raw[:], in_=w_rows)
         nc.sync.dma_start(out=x_raw[1][:], in_=x_rows[1])
-
-        nc.vector.memset(b_blocks[:], 0.0)
-        for q in range(P // QUAD):
-            nc.scalar.dma_start(
-                out=b_blocks[QUAD * q : QUAD * q + G, :],
-                in_=b_rows[:, QUAD * q : QUAD * (q + 1)],
-            )
-
         for k in range(G // PAIR):
             nc.sync.dma_start(out=r_sb[k][:], in_=r_rows[:, PAIR * k : PAIR * (k + 1), :])
 
@@ -106,16 +100,15 @@ def tile_rows_glin_relu_bias_res_kernel(tc, x, w, b, r, out):
         for s in range(SETS):
             interleave(nc.scalar.copy, w_bf[s], w_raw[:, s, :, :], all_m)
         quantize(w_codes[0], w_scales[0], w_bf[0])
-        nc.vector.transpose(out=bias[:], in_=b_blocks[:])
+        nc.vector.transpose(out=bias[:].rearrange("p g i -> p (g i)"), in_=b_blocks[:].rearrange("p g i -> p (g i)"))
         quantize(w_codes[1], w_scales[1], w_bf[1])
         products(0)
-        bias_relu(0)
 
         interleave(nc.vector.tensor_copy, x_bf[1], x_raw[1], vector_cols)
         interleave(nc.scalar.copy, x_bf[1], x_raw[1], scalar_cols)
         quantize(x_codes[1], x_scales[1], x_bf[1])
         products(1)
-        for g in range(1, G):
+        for g in range(G):
             bias_relu(g)
 
         for g in range(G):

@@ -20,7 +20,8 @@ SIDE = P // ROWS
 SETS = G // SIDE
 QUAD = 32
 RUN = 4
-X_VECTOR_COLS = 344
+X_VECTOR_COLS = 312
+STORES = ((0, 2), (2, 4), (4, 6), (6, 8))
 PAIR = 2
 
 
@@ -34,7 +35,7 @@ def interleave(copy, grouped, raw, cols):
 def tile_rows_glin_relu_bias_res_kernel(tc, x, w, b, r, out):
     nc = tc.nc
     x_rows = x.flatten_outer_dims().rearrange("(s q j) n -> s q j n", s=SETS, j=PACK)
-    w_rows = w.flatten_outer_dims().rearrange("(s q j) m -> q s j m", s=SETS, j=PACK)
+    w_rows = w.flatten_outer_dims().rearrange("(s q j) m -> s q j m", s=SETS, j=PACK)
     b_rows = b.rearrange("g (q i) one -> q g (i one)", i=QUAD)
     r_rows = r.rearrange("g m n -> m g n")
     out_rows = out.rearrange("g m n -> m g n")
@@ -48,7 +49,7 @@ def tile_rows_glin_relu_bias_res_kernel(tc, x, w, b, r, out):
         x_bf = [sb.tile([P, N, PACK], BF16, name="x_bf%d" % s, align_bytes=64) for s in range(SETS)]
         x_codes = [sb.tile([P, N], U32, name="x_codes%d" % s, align_bytes=64) for s in range(SETS)]
         x_scales = [sb.tile([P, N], U8, name="x_scales%d" % s, align_bytes=64) for s in range(SETS)]
-        w_raw = sb.tile([P, SETS, PACK, M], F32, align_bytes=64)
+        w_raw = [sb.tile([P, PACK, M], F32, name="w_raw%d" % s, align_bytes=64) for s in range(SETS)]
         w_bf = [sb.tile([P, M, PACK], BF16, name="w_bf%d" % s, align_bytes=64) for s in range(SETS)]
         w_codes = [sb.tile([P, M], U32, name="w_codes%d" % s, align_bytes=64) for s in range(SETS)]
         w_scales = [sb.tile([P, M], U8, name="w_scales%d" % s, align_bytes=64) for s in range(SETS)]
@@ -56,7 +57,7 @@ def tile_rows_glin_relu_bias_res_kernel(tc, x, w, b, r, out):
         bias = sb.tile([P, G, QUAD], F32, align_bytes=64)
         r_sb = [sb.tile([P, PAIR, N], F32, name="r_sb%d" % k, align_bytes=64) for k in range(G // PAIR)]
         act = [sb.tile([P, N], F32, name="act%d" % g, align_bytes=64) for g in range(G)]
-        res = [sb.tile([P, PAIR, N], F32, name="res%d" % k, align_bytes=64) for k in range(G // PAIR)]
+        res = [sb.tile([P, hi - lo, N], F32, name="res%d" % lo, align_bytes=64) for lo, hi in STORES]
         acc = [psum.tile([M, N], F32, name="acc%d" % g) for g in range(G)]
 
         def quantize(codes, scales, grouped):
@@ -89,30 +90,31 @@ def tile_rows_glin_relu_bias_res_kernel(tc, x, w, b, r, out):
         nc.vector.memset(b_blocks[:], 0.0)
         nc.sync.dma_start(out=x_raw[0][:], in_=x_rows[0])
         nc.sync.dma_start(out=b_blocks[0:P:QUAD, :, :], in_=b_rows)
-        nc.sync.dma_start(out=w_raw[:], in_=w_rows)
+        nc.sync.dma_start(out=w_raw[0][:], in_=w_rows[0])
         nc.sync.dma_start(out=x_raw[1][:], in_=x_rows[1])
+        nc.sync.dma_start(out=w_raw[1][:], in_=w_rows[1])
         for k in range(G // PAIR):
             nc.sync.dma_start(out=r_sb[k][:], in_=r_rows[:, PAIR * k : PAIR * (k + 1), :])
 
         interleave(nc.vector.tensor_copy, x_bf[0], x_raw[0], vector_cols)
         interleave(nc.scalar.copy, x_bf[0], x_raw[0], scalar_cols)
         quantize(x_codes[0], x_scales[0], x_bf[0])
-        for s in range(SETS):
-            interleave(nc.scalar.copy, w_bf[s], w_raw[:, s, :, :], all_m)
+        interleave(nc.scalar.copy, w_bf[0], w_raw[0], all_m)
         quantize(w_codes[0], w_scales[0], w_bf[0])
         nc.vector.transpose(out=bias[:].rearrange("p g i -> p (g i)"), in_=b_blocks[:].rearrange("p g i -> p (g i)"))
-        quantize(w_codes[1], w_scales[1], w_bf[1])
         products(0)
 
         interleave(nc.vector.tensor_copy, x_bf[1], x_raw[1], vector_cols)
         interleave(nc.scalar.copy, x_bf[1], x_raw[1], scalar_cols)
+        interleave(nc.vector.tensor_copy, w_bf[1], w_raw[1], all_m)
         quantize(x_codes[1], x_scales[1], x_bf[1])
+        quantize(w_codes[1], w_scales[1], w_bf[1])
         products(1)
         for g in range(G):
             bias_relu(g)
 
-        for g in range(G):
-            k, e = divmod(g, PAIR)
-            nc.vector.tensor_tensor(out=res[k][:, e, :], in0=act[g][:], in1=r_sb[k][:, e, :], op=ADD)
-            if e == PAIR - 1:
-                nc.sync.dma_start(out=out_rows[:, PAIR * k : PAIR * (k + 1), :], in_=res[k][:])
+        for tile, (lo, hi) in zip(res, STORES):
+            for g in range(lo, hi):
+                k, e = divmod(g, PAIR)
+                nc.vector.tensor_tensor(out=tile[:, g - lo, :], in0=act[g][:], in1=r_sb[k][:, e, :], op=ADD)
+            nc.sync.dma_start(out=out_rows[:, lo:hi, :], in_=tile[:])

from contextlib import ExitStack

import concourse.mybir as mybir

G, D, M, N = 8, 128, 128, 512
FLOPS = 2 * G * D * M * N

F32 = mybir.dt.float32
BF16 = mybir.dt.bfloat16
U32 = mybir.dt.uint32
U8 = mybir.dt.uint8
FP8X4 = mybir.dt.float8_e4m3fn_x4
RELU = mybir.ActivationFunctionType.Relu
ADD = mybir.AluOpType.add

P = 128
PACK = 4
ROWS = D // PACK
SIDE = P // ROWS
SETS = G // SIDE
QUAD = 32
RUN = 4
X_VECTOR_COLS = 312
STORES = ((0, 2), (2, 4), (4, 6), (6, 8))
PAIR = 2


def interleave(copy, grouped, raw, cols):
    copy(
        out=grouped[:, cols, :].rearrange("p (c i) j -> p c j i", i=RUN),
        in_=raw[:, :, cols].rearrange("p j (c i) -> p c j i", i=RUN),
    )


def tile_rows_glin_relu_bias_res_kernel(tc, x, w, b, r, out):
    nc = tc.nc
    x_rows = x.flatten_outer_dims().rearrange("(s q j) n -> s q j n", s=SETS, j=PACK)
    w_rows = w.flatten_outer_dims().rearrange("(s q j) m -> s q j m", s=SETS, j=PACK)
    b_rows = b.rearrange("g (q i) one -> q g (i one)", i=QUAD)
    r_rows = r.rearrange("g m n -> m g n")
    out_rows = out.rearrange("g m n -> m g n")

    with ExitStack() as ctx:
        sb = ctx.enter_context(tc.tile_pool(name="sb", bufs=1))
        psum = ctx.enter_context(tc.psum_pool(name="psum", bufs=1))
        ctx.enter_context(tc.manual_schedule())

        x_raw = [sb.tile([P, PACK, N], F32, name="x_raw%d" % s, align_bytes=64) for s in range(SETS)]
        x_bf = [sb.tile([P, N, PACK], BF16, name="x_bf%d" % s, align_bytes=64) for s in range(SETS)]
        x_codes = [sb.tile([P, N], U32, name="x_codes%d" % s, align_bytes=64) for s in range(SETS)]
        x_scales = [sb.tile([P, N], U8, name="x_scales%d" % s, align_bytes=64) for s in range(SETS)]
        w_raw = [sb.tile([P, PACK, M], F32, name="w_raw%d" % s, align_bytes=64) for s in range(SETS)]
        w_bf = [sb.tile([P, M, PACK], BF16, name="w_bf%d" % s, align_bytes=64) for s in range(SETS)]
        w_codes = [sb.tile([P, M], U32, name="w_codes%d" % s, align_bytes=64) for s in range(SETS)]
        w_scales = [sb.tile([P, M], U8, name="w_scales%d" % s, align_bytes=64) for s in range(SETS)]
        b_blocks = sb.tile([P, G, QUAD], F32, align_bytes=64)
        bias = sb.tile([P, G, QUAD], F32, align_bytes=64)
        r_sb = [sb.tile([P, PAIR, N], F32, name="r_sb%d" % k, align_bytes=64) for k in range(G // PAIR)]
        act = [sb.tile([P, N], F32, name="act%d" % g, align_bytes=64) for g in range(G)]
        res = [sb.tile([P, hi - lo, N], F32, name="res%d" % lo, align_bytes=64) for lo, hi in STORES]
        acc = [psum.tile([M, N], F32, name="acc%d" % g) for g in range(G)]

        def quantize(codes, scales, grouped):
            nc.vector.quantize_mx(
                out=codes[:].bitcast(FP8X4),
                scales=scales[:],
                in_=grouped[:].rearrange("p c j -> p (c j)"),
            )

        def products(s):
            for c in range(SIDE):
                rows = slice(ROWS * c, ROWS * (c + 1))
                nc.tensor.matmul_mx(
                    out=acc[SIDE * s + c][:],
                    lhsT=w_codes[s][rows, :].bitcast(FP8X4),
                    lhsT_scale=w_scales[s][rows, :],
                    rhs=x_codes[s][rows, :].bitcast(FP8X4),
                    rhs_scale=x_scales[s][rows, :],
                    start=True,
                    stop=True,
                )

        def bias_relu(g):
            nc.scalar.activation(out=act[g][:], in_=acc[g][:], func=RELU, bias=bias[:, g, 0:1])

        vector_cols = slice(0, X_VECTOR_COLS)
        scalar_cols = slice(X_VECTOR_COLS, N)
        all_m = slice(0, M)

        nc.vector.memset(b_blocks[:], 0.0)
        nc.sync.dma_start(out=x_raw[0][:], in_=x_rows[0])
        nc.sync.dma_start(out=b_blocks[0:P:QUAD, :, :], in_=b_rows)
        nc.sync.dma_start(out=w_raw[0][:], in_=w_rows[0])
        nc.sync.dma_start(out=x_raw[1][:], in_=x_rows[1])
        nc.sync.dma_start(out=w_raw[1][:], in_=w_rows[1])
        for k in range(G // PAIR):
            nc.sync.dma_start(out=r_sb[k][:], in_=r_rows[:, PAIR * k : PAIR * (k + 1), :])

        interleave(nc.vector.tensor_copy, x_bf[0], x_raw[0], vector_cols)
        interleave(nc.scalar.copy, x_bf[0], x_raw[0], scalar_cols)
        quantize(x_codes[0], x_scales[0], x_bf[0])
        interleave(nc.scalar.copy, w_bf[0], w_raw[0], all_m)
        quantize(w_codes[0], w_scales[0], w_bf[0])
        nc.vector.transpose(out=bias[:].rearrange("p g i -> p (g i)"), in_=b_blocks[:].rearrange("p g i -> p (g i)"))
        products(0)

        interleave(nc.vector.tensor_copy, x_bf[1], x_raw[1], vector_cols)
        interleave(nc.scalar.copy, x_bf[1], x_raw[1], scalar_cols)
        interleave(nc.vector.tensor_copy, w_bf[1], w_raw[1], all_m)
        quantize(x_codes[1], x_scales[1], x_bf[1])
        quantize(w_codes[1], w_scales[1], w_bf[1])
        products(1)
        for g in range(G):
            bias_relu(g)

        for tile, (lo, hi) in zip(res, STORES):
            for g in range(lo, hi):
                k, e = divmod(g, PAIR)
                nc.vector.tensor_tensor(out=tile[:, g - lo, :], in0=act[g][:], in1=r_sb[k][:, e, :], op=ADD)
            nc.sync.dma_start(out=out_rows[:, lo:hi, :], in_=tile[:])
